import numpy as np
import ml_dtypes


def mxq(x, axis, fmt="e4m3"):
    dtype, down = {"e4m3": (ml_dtypes.float8_e4m3fn, 7), "e5m2": (ml_dtypes.float8_e5m2, 14)}[fmt]
    v = np.moveaxis(np.asarray(x, np.float32).astype(ml_dtypes.bfloat16).astype(np.float64), axis, -1)
    blocks = v.reshape(v.shape[:-1] + (-1, 32))
    amax = np.abs(blocks).max(-1, keepdims=True)
    byte = np.maximum(np.where(amax > 0, np.frexp(amax)[1] - 1 + 127, 0) - down, 1)
    scale = np.exp2(byte - 127.0)
    codes = (blocks / scale).astype(np.float32).astype(dtype).astype(np.float64)
    return np.moveaxis((codes * scale).reshape(v.shape), -1, axis)


WIDE = False


def mx_kscale(k):
    if not WIDE:
        return np.ones(k)
    levels = np.array([10, -10, 5, -5, 0])
    if k % 512:
        return np.exp2(np.random.permutation(np.resize(levels, k // 32))).repeat(32)
    a = np.empty((k // 512, 16))
    for p in range(k // 512):
        a[p, :8] = np.random.permutation(np.resize(levels, 8))
        for g in range(8):
            far = levels[np.abs(levels - a[p, g]) >= 10]
            a[p, g + 8] = far[np.random.randint(len(far))]
    return np.exp2(a.ravel()).repeat(32)


def f64(x):
    return np.asarray(x).astype(np.float64)


def striped8(idx):
    return np.asarray(idx).reshape(8, -1, 16).transpose(0, 2, 1).reshape(128, -1).astype(np.uint16)


def unstriped8(offs):
    return offs.reshape(8, 16, -1).transpose(0, 2, 1).reshape(8, -1).astype(np.int64)


def pick8(x, idx, run):
    r = np.arange(len(x))
    return x[r[:, None], idx[r % (8 * run) // run]]


E2M1 = np.array([0.0, 0.5, 1.0, 1.5, 2.0, 3.0, 4.0, 6.0, -0.0, -0.5, -1.0, -1.5, -2.0, -3.0, -4.0, -6.0])


def pack_weight(w, fmt):
    k, n = w.shape
    w = f64(np.asarray(w, np.float32).astype(ml_dtypes.bfloat16)).reshape(k // 32, 32, n)
    amax = np.abs(w).max(1)
    if fmt == "e4m3":
        byte = np.frexp(amax)[1] - 1 + 127 - 7
    else:
        mant, ex = np.frexp(amax / 6.0)
        byte = np.where(mant > 0.5, ex, ex - 1) + 127
    byte = np.clip(np.where(amax > 0, byte, 1), 1, 254)
    scaled = (w * np.exp2(127.0 - byte)[:, None, :]).reshape(k, n).astype(np.float32)
    by_word = np.ascontiguousarray(scaled.reshape(k // 512, 128, 4, n).transpose(0, 1, 3, 2))
    if fmt == "e4m3":
        words = by_word.astype(ml_dtypes.float8_e4m3fn).view(np.uint8)
    else:
        c = by_word.astype(ml_dtypes.float4_e2m1fn).view(np.uint8) & 0xF
        words = (c[..., 0::2] | (c[..., 1::2] << 4)).reshape(k // 512, 128, 2 * n)
    return np.ascontiguousarray(words), np.ascontiguousarray(byte.astype(np.uint8).reshape(k // 512, 16, n))


def unpack_weight(words, scales, fmt):
    g, _, n = scales.shape
    words = np.ascontiguousarray(words).reshape(g, 128, n, -1)
    if fmt == "e4m3":
        vals = words.view(ml_dtypes.float8_e4m3fn).astype(np.float64)
    else:
        nib = np.empty((g, 128, n, 4), np.uint8)
        nib[..., 0::2] = words & 0xF
        nib[..., 1::2] = words >> 4
        vals = E2M1[nib]
    vals = vals * np.repeat(np.exp2(scales.astype(np.float64) - 127.0), 8, axis=1)[..., None]
    return vals.transpose(0, 1, 3, 2).reshape(g * 512, n)


D, T, U, X, S, I, Q = 512, 1024, 1024, 1024, 1024, 512, 128


def setup_inputs():
    n = np.random.standard_normal
    idx = np.stack([np.random.permutation(T)[:I] for _ in range(8)])
    idx2 = np.stack([np.random.permutation(U)[:I] for _ in range(8)])
    idx3 = np.stack([np.random.permutation(X)[:I] for _ in range(8)])
    idx4 = np.stack([np.random.permutation(S)[:I] for _ in range(8)])
    idx5 = np.stack([np.random.permutation(T)[:I] for _ in range(8)])
    idx6 = np.stack([np.random.permutation(S)[:I] for _ in range(8)])
    fd = mx_kscale(D)
    keysp = pack_weight(n((D, T)) / fd[:, None], "e2m1")
    notesp = pack_weight(n((D, U)) / fd[:, None], "e4m3")
    usersp = pack_weight(n((D, X)) / fd[:, None], "e2m1")
    shelvesp = pack_weight(n((D, S)) / fd[:, None], "e4m3")
    return {
        "query": (n((D, Q)) * 1.0 / np.sqrt(D) * fd[:, None]).astype(np.float32),
        "keys_words": keysp[0],
        "keys_scales": keysp[1],
        "notes_words": notesp[0],
        "notes_scales": notesp[1],
        "users_words": usersp[0],
        "users_scales": usersp[1],
        "shelves_words": shelvesp[0],
        "shelves_scales": shelvesp[1],
        "offs": striped8(idx),
        "offs2": striped8(idx2),
        "offs3": striped8(idx3),
        "offs4": striped8(idx4),
        "offs5": striped8(idx5),
        "offs6": striped8(idx6),
    }


def reference(query, keys_words, keys_scales, notes_words, notes_scales, users_words, users_scales, shelves_words, shelves_scales, offs, offs2, offs3, offs4, offs5, offs6):
    idx = unstriped8(offs)
    idx2 = unstriped8(offs2)
    idx3 = unstriped8(offs3)
    idx4 = unstriped8(offs4)
    idx5 = unstriped8(offs5)
    idx6 = unstriped8(offs6)
    keysu = unpack_weight(keys_words, keys_scales, "e2m1")
    notesu = unpack_weight(notes_words, notes_scales, "e4m3")
    usersu = unpack_weight(users_words, users_scales, "e2m1")
    shelvesu = unpack_weight(shelves_words, shelves_scales, "e4m3")
    queryq = mxq(f64(query), 0, "e4m3")
    a = queryq.T @ keysu
    b = queryq.T @ notesu
    c0 = queryq.T @ usersu
    d0 = queryq.T @ shelvesu
    hi1 = np.maximum(pick8(a, idx, 16), pick8(b, idx2, 16))
    hi2 = np.maximum(pick8(c0, idx3, 16), pick8(d0, idx4, 16))
    r = np.minimum(hi1, hi2)
    f1 = np.zeros((Q, T))
    f1[np.arange(Q)[:, None], idx[np.arange(Q) % 128 // 16]] = r
    f2 = np.zeros((Q, S))
    f2[np.arange(Q)[:, None], idx4[np.arange(Q) % 128 // 16]] = r
    aa = a - f1
    dd = d0 + f2
    y = pick8(aa, idx5, 16) + pick8(dd, idx6, 16)
    return y

@@ -1,0 +1,152 @@
+from contextlib import ExitStack
+
+import concourse.mybir as mybir
+
+F32 = mybir.dt.float32
+BF16 = mybir.dt.bfloat16
+I32 = mybir.dt.int32
+U32 = mybir.dt.uint32
+U16 = mybir.dt.uint16
+U8 = mybir.dt.uint8
+FP8X4 = mybir.dt.float8_e4m3fn_x4
+FP4X4 = mybir.dt.float4_e2m1fn_x4
+ALU = mybir.AluOpType
+COPY = mybir.ActivationFunctionType.Copy
+
+P = 128
+PACK = 4
+D, COLS, SLOTS, Q = 512, 1024, 512, 128
+BANK = 512
+HALF = SLOTS // 2
+FLOPS = 4 * 2 * D * Q * COLS
+
+
+def tile_attend_quartet_four_kernel(tc, query, keys_words, keys_scales, notes_words, notes_scales,
+                                     users_words, users_scales, shelves_words, shelves_scales,
+                                     offs, offs2, offs3, offs4, offs5, offs6, out):
+    nc = tc.nc
+    with ExitStack() as ctx:
+        sb = ctx.enter_context(tc.tile_pool(name="sb", bufs=1))
+        ps = ctx.enter_context(tc.psum_pool(name="ps", bufs=1))
+
+        pools = [
+            ("a", keys_words[0], keys_scales[0], FP4X4, 2, 0),
+            ("b", notes_words[0].rearrange("p n t -> p (n t)"), notes_scales[0], FP8X4, 4, 4),
+            ("d", shelves_words[0].rearrange("p n t -> p (n t)"), shelves_scales[0], FP8X4, 4, 8),
+            ("c", users_words[0], users_scales[0], FP4X4, 2, 0),
+        ]
+        planes = {}
+        words = {}
+        for name, w_in, s_in, fmt, width, row0 in pools:
+            planes[name] = sb.tile([P, COLS], U8, name="plane_" + name, align_bytes=64)
+            words[name] = sb.tile([P, width * COLS], U8, name="words_" + name, align_bytes=64)
+            nc.vector.memset(planes[name][:].bitcast(I32), 0)
+        f1 = sb.tile([P, COLS], F32, name="f1")
+        f2 = sb.tile([P, COLS], F32, name="f2")
+        nc.vector.memset(f1[:], 0.0)
+        nc.vector.memset(f2[:], 0.0)
+
+        lists = {}
+        list_in = {"a": offs, "b": offs2, "c": offs3, "d": offs4, "aa": offs5, "dd": offs6}
+        for name in list_in:
+            lists[name] = sb.tile([P, SLOTS // 16], U16, name="list_" + name)
+
+        def half(name, h):
+            return lists[name][:, h * (HALF // 16):(h + 1) * (HALF // 16)]
+
+        q_raw = sb.tile([P, PACK, Q], F32, name="q_raw")
+        nc.sync.dma_start(out=q_raw[:], in_=query.rearrange("(p t) q -> p t q", t=PACK))
+
+        def load_words(name, w_in):
+            nc.sync.dma_start(out=words[name][:].bitcast(I32), in_=w_in.bitcast(I32))
+
+        def load_scales(name, s_in, row0):
+            rows = s_in.rearrange("(g r) n -> r g n", r=4)
+            for r in range(4):
+                nc.sync.dma_start(out=planes[name][row0 + r:P:32, :].bitcast(I32), in_=rows[r].bitcast(I32))
+
+        before = None
+        for name, w_in, s_in, fmt, width, row0 in pools:
+            if before is None:
+                load_scales(name, s_in, row0)
+                load_words(name, w_in)
+            else:
+                load_words(name, w_in)
+                nc.sync.dma_start(lists[before][:], list_in[before])
+                load_scales(name, s_in, row0)
+            before = name
+        for name in (before, "aa", "dd"):
+            nc.sync.dma_start(lists[name][:], list_in[name])
+
+        q_grp = sb.tile([P, Q, PACK], BF16, name="q_grp", align_bytes=64)
+        q_codes = sb.tile([P, Q], U32, name="q_codes", align_bytes=64)
+        q_plane = sb.tile([P, Q], U8, name="q_plane", align_bytes=64)
+        nc.vector.tensor_copy(out=q_grp[:], in_=q_raw[:].rearrange("p t q -> p q t"))
+        nc.vector.quantize_mx(out=q_codes[:].bitcast(FP8X4), scales=q_plane[:],
+                              in_=q_grp[:].rearrange("p q t -> p (q t)"))
+
+        score = {}
+        picked = {}
+        banks = {}
+        for name, w_in, s_in, fmt, width, row0 in pools:
+            score[name] = sb.tile([P, COLS], F32, name="score_" + name)
+            picked[name] = sb.tile([P, SLOTS], F32, name="picked_" + name)
+            for j in range(2):
+                banks[name, j] = ps.tile([P, BANK], F32, name="bank_%s%d" % (name, j))
+                nc.tensor.matmul_mx(
+                    out=banks[name, j][:],
+                    lhsT=q_codes[:].bitcast(FP8X4), lhsT_scale=q_plane[:],
+                    rhs=words[name][:, width * BANK * j:width * BANK * (j + 1)].bitcast(fmt),
+                    rhs_scale=planes[name][row0:P, BANK * j:BANK * (j + 1)],
+                    start=True, stop=True)
+
+        def empty(name, j, on_vector):
+            dst = score[name][:, BANK * j:BANK * (j + 1)]
+            if on_vector:
+                nc.vector.tensor_copy(out=dst, in_=banks[name, j][:])
+            else:
+                nc.scalar.activation(out=dst, in_=banks[name, j][:], func=COPY)
+
+        def pick(name, h, on_vector):
+            dst = picked[name][:, HALF * h:HALF * (h + 1)]
+            src = score[name][:].indirect(half(name, h))
+            if on_vector:
+                nc.vector.tensor_copy(out=dst, in_=src)
+            else:
+                nc.scalar.activation(out=dst, in_=src, func=COPY)
+
+        hi1 = sb.tile([P, SLOTS], F32, name="hi1")
+        hi2 = sb.tile([P, SLOTS], F32, name="hi2")
+        r = sb.tile([P, SLOTS], F32, name="r")
+
+        def cols(t, h):
+            return t[:, HALF * h:HALF * (h + 1)]
+
+        for name in "abdc":
+            empty(name, 0, True)
+            empty(name, 1, False)
+            pick(name, 0, True)
+            pick(name, 1, False)
+            if name == "b":
+                nc.vector.tensor_tensor(hi1[:], picked["a"][:], picked["b"][:], ALU.max)
+        for h in range(2):
+            nc.vector.tensor_tensor(cols(hi2, h), cols(picked["c"], h), cols(picked["d"], h), ALU.max)
+        for h in range(2):
+            nc.vector.tensor_tensor(cols(r, h), cols(hi1, h), cols(hi2, h), ALU.min)
+        nc.vector.tensor_copy(out=f1[:].indirect(lists["a"][:]), in_=r[:])
+        nc.vector.tensor_copy(out=f2[:].indirect(lists["d"][:]), in_=r[:])
+
+        aa = sb.tile([P, COLS], F32, name="aa")
+        dd = sb.tile([P, COLS], F32, name="dd")
+        left = sb.tile([P, SLOTS], F32, name="left")
+        stand = sb.tile([P, HALF], F32, name="stand")
+        y0 = sb.tile([P, HALF], F32, name="y0")
+        y1 = sb.tile([P, HALF], F32, name="y1")
+        nc.gpsimd.tensor_tensor(aa[:], score["a"][:], f1[:], ALU.subtract)
+        nc.scalar.activation(out=left[:], in_=aa[:].indirect(lists["aa"][:]), func=COPY)
+        nc.vector.tensor_tensor(dd[:], score["d"][:], f2[:], ALU.add)
+        nc.vector.tensor_tensor(y0[:], dd[:].indirect(half("dd", 0)), cols(left, 0), ALU.add)
+        nc.scalar.activation(out=stand[:], in_=dd[:].indirect(half("dd", 1)), func=COPY)
+        nc.vector.tensor_tensor(y1[:], stand[:], cols(left, 1), ALU.add)
+        nc.sync.dma_start(out=out[:, 0:HALF], in_=y0[:])
+        nc.scalar.dma_start(out=out[:, HALF:SLOTS], in_=y1[:])

@@ -29,22 +29,20 @@ def tile_attend_quartet_four_kernel(tc, query, keys_words, keys_scales, notes_wo
         sb = ctx.enter_context(tc.tile_pool(name="sb", bufs=1))
         ps = ctx.enter_context(tc.psum_pool(name="ps", bufs=1))
 
-        pools = [
-            ("a", keys_words[0], keys_scales[0], FP4X4, 2, 0),
-            ("b", notes_words[0].rearrange("p n t -> p (n t)"), notes_scales[0], FP8X4, 4, 4),
-            ("d", shelves_words[0].rearrange("p n t -> p (n t)"), shelves_scales[0], FP8X4, 4, 8),
-            ("c", users_words[0], users_scales[0], FP4X4, 2, 0),
-        ]
+        pools = {
+            "a": (keys_words[0], keys_scales[0], FP4X4, 2, 0),
+            "b": (notes_words[0].rearrange("p n t -> p (n t)"), notes_scales[0], FP8X4, 4, 4),
+            "c": (users_words[0], users_scales[0], FP4X4, 2, 0),
+            "d": (shelves_words[0].rearrange("p n t -> p (n t)"), shelves_scales[0], FP8X4, 4, 8),
+        }
         planes = {}
         words = {}
-        for name, w_in, s_in, fmt, width, row0 in pools:
+        for name in "abdc":
             planes[name] = sb.tile([P, COLS], U8, name="plane_" + name, align_bytes=64)
-            words[name] = sb.tile([P, width * COLS], U8, name="words_" + name, align_bytes=64)
+            words[name] = sb.tile([P, pools[name][3] * COLS], U8, name="words_" + name, align_bytes=64)
             nc.vector.memset(planes[name][:].bitcast(I32), 0)
         f1 = sb.tile([P, COLS], F32, name="f1")
-        f2 = sb.tile([P, COLS], F32, name="f2")
         nc.vector.memset(f1[:], 0.0)
-        nc.vector.memset(f2[:], 0.0)
 
         lists = {}
         list_in = {"a": offs, "b": offs2, "c": offs3, "d": offs4, "aa": offs5, "dd": offs6}
@@ -54,79 +52,66 @@ def tile_attend_quartet_four_kernel(tc, query, keys_words, keys_scales, notes_wo
         def half(name, h):
             return lists[name][:, h * (HALF // 16):(h + 1) * (HALF // 16)]
 
+        def load_words(name):
+            nc.sync.dma_start(out=words[name][:].bitcast(I32), in_=pools[name][0].bitcast(I32))
+
+        def load_scales(name, queue):
+            rows = pools[name][1].rearrange("(g r) n -> r g n", r=4)
+            row0 = pools[name][4]
+            for r in range(4):
+                queue.dma_start(out=planes[name][row0 + r:P:32, :].bitcast(I32), in_=rows[r].bitcast(I32))
+
         q_raw = sb.tile([P, PACK, Q], F32, name="q_raw")
         nc.sync.dma_start(out=q_raw[:], in_=query.rearrange("(p t) q -> p t q", t=PACK))
-
-        def load_words(name, w_in):
-            nc.sync.dma_start(out=words[name][:].bitcast(I32), in_=w_in.bitcast(I32))
-
-        def load_scales(name, s_in, row0):
-            rows = s_in.rearrange("(g r) n -> r g n", r=4)
-            for r in range(4):
-                nc.sync.dma_start(out=planes[name][row0 + r:P:32, :].bitcast(I32), in_=rows[r].bitcast(I32))
-
-        before = None
-        for name, w_in, s_in, fmt, width, row0 in pools:
-            if before is None:
-                load_scales(name, s_in, row0)
-                load_words(name, w_in)
-            else:
-                load_words(name, w_in)
-                nc.sync.dma_start(lists[before][:], list_in[before])
-                load_scales(name, s_in, row0)
-            before = name
-        for name in (before, "aa", "dd"):
+        load_scales("a", nc.sync)
+        load_words("a")
+        for before, name in zip("abd", "bdc"):
+            load_words(name)
+            load_scales(name, nc.sync)
+            nc.sync.dma_start(lists[before][:], list_in[before])
+        for name in ("c", "aa", "dd"):
             nc.sync.dma_start(lists[name][:], list_in[name])
 
-        q_grp = sb.tile([P, Q, PACK], BF16, name="q_grp", align_bytes=64)
+        q_grp = sb.tile([P, Q, PACK], BF16, name="q_grp", tag="q_grp_f2", align_bytes=64)
         q_codes = sb.tile([P, Q], U32, name="q_codes", align_bytes=64)
         q_plane = sb.tile([P, Q], U8, name="q_plane", align_bytes=64)
         nc.vector.tensor_copy(out=q_grp[:], in_=q_raw[:].rearrange("p t q -> p q t"))
         nc.vector.quantize_mx(out=q_codes[:].bitcast(FP8X4), scales=q_plane[:],
                               in_=q_grp[:].rearrange("p q t -> p (q t)"))
-
-        score = {}
-        picked = {}
-        banks = {}
-        for name, w_in, s_in, fmt, width, row0 in pools:
-            score[name] = sb.tile([P, COLS], F32, name="score_" + name)
-            picked[name] = sb.tile([P, SLOTS], F32, name="picked_" + name)
-            for j in range(2):
-                banks[name, j] = ps.tile([P, BANK], F32, name="bank_%s%d" % (name, j))
-                nc.tensor.matmul_mx(
-                    out=banks[name, j][:],
-                    lhsT=q_codes[:].bitcast(FP8X4), lhsT_scale=q_plane[:],
-                    rhs=words[name][:, width * BANK * j:width * BANK * (j + 1)].bitcast(fmt),
-                    rhs_scale=planes[name][row0:P, BANK * j:BANK * (j + 1)],
-                    start=True, stop=True)
-
-        def empty(name, j, on_vector):
-            dst = score[name][:, BANK * j:BANK * (j + 1)]
-            if on_vector:
-                nc.vector.tensor_copy(out=dst, in_=banks[name, j][:])
-            else:
-                nc.scalar.activation(out=dst, in_=banks[name, j][:], func=COPY)
-
-        def pick(name, h, on_vector):
-            dst = picked[name][:, HALF * h:HALF * (h + 1)]
-            src = score[name][:].indirect(half(name, h))
-            if on_vector:
-                nc.vector.tensor_copy(out=dst, in_=src)
-            else:
-                nc.scalar.activation(out=dst, in_=src, func=COPY)
-
-        hi1 = sb.tile([P, SLOTS], F32, name="hi1")
-        hi2 = sb.tile([P, SLOTS], F32, name="hi2")
-        r = sb.tile([P, SLOTS], F32, name="r")
+        f2 = sb.tile([P, COLS], F32, name="f2", tag="q_grp_f2", align_bytes=64)
+        nc.vector.memset(f2[:], 0.0)
 
         def cols(t, h):
             return t[:, HALF * h:HALF * (h + 1)]
 
+        score = {}
+        picked = {}
+        hi1 = sb.tile([P, SLOTS], F32, name="hi1")
+        hi2 = sb.tile([P, SLOTS], F32, name="hi2")
+        r = sb.tile([P, SLOTS], F32, name="r")
+        banks = {}
+        bank_tags = {"a": (0, 1), "b": (2, 3), "d": (4, 5), "c": (6, 7, 0, 1)}
         for name in "abdc":
-            empty(name, 0, True)
-            empty(name, 1, False)
-            pick(name, 0, True)
-            pick(name, 1, False)
+            w_in, s_in, fmt, width, row0 = pools[name]
+            score[name] = sb.tile([P, COLS], F32, name="score_" + name)
+            picked[name] = sb.tile([P, SLOTS], F32, name="picked_" + name)
+            n = COLS // len(bank_tags[name])
+            for j, tag in enumerate(bank_tags[name]):
+                bank = ps.tile([P, n], F32, name="bank", tag="bank_%d" % tag)
+                banks[name, j] = bank
+                nc.tensor.matmul_mx(
+                    out=bank[:],
+                    lhsT=q_codes[:].bitcast(FP8X4), lhsT_scale=q_plane[:],
+                    rhs=words[name][:, width * n * j:width * n * (j + 1)].bitcast(fmt),
+                    rhs_scale=planes[name][row0:P, n * j:n * (j + 1)],
+                    start=True, stop=True)
+                dst = score[name][:, n * j:n * (j + 1)]
+                if j % 2 == 0:
+                    nc.vector.tensor_copy(out=dst, in_=bank[:])
+                else:
+                    nc.scalar.activation(out=dst, in_=bank[:], func=COPY)
+            nc.vector.tensor_copy(out=cols(picked[name], 0), in_=score[name][:].indirect(half(name, 0)))
+            nc.scalar.activation(out=cols(picked[name], 1), in_=score[name][:].indirect(half(name, 1)), func=COPY)
             if name == "b":
                 nc.vector.tensor_tensor(hi1[:], picked["a"][:], picked["b"][:], ALU.max)
         for h in range(2):
@@ -144,7 +129,10 @@ def tile_attend_quartet_four_kernel(tc, query, keys_words, keys_scales, notes_wo
         y1 = sb.tile([P, HALF], F32, name="y1")
         nc.gpsimd.tensor_tensor(aa[:], score["a"][:], f1[:], ALU.subtract)
         nc.scalar.activation(out=left[:], in_=aa[:].indirect(lists["aa"][:]), func=COPY)
-        nc.vector.tensor_tensor(dd[:], score["d"][:], f2[:], ALU.add)
+        cut = 768
+        nc.gpsimd.tensor_tensor(dd[:, cut:], score["d"][:, cut:], f2[:, cut:], ALU.add)
+        nc.vector.tensor_tensor(dd[:, :BANK], banks["d", 0][:], f2[:, :BANK], ALU.add)
+        nc.vector.tensor_tensor(dd[:, BANK:cut], banks["d", 1][:, :cut - BANK], f2[:, BANK:cut], ALU.add)
         nc.vector.tensor_tensor(y0[:], dd[:].indirect(half("dd", 0)), cols(left, 0), ALU.add)
         nc.scalar.activation(out=stand[:], in_=dd[:].indirect(half("dd", 1)), func=COPY)
         nc.vector.tensor_tensor(y1[:], stand[:], cols(left, 1), ALU.add)

@@ -118,8 +118,10 @@ def tile_attend_quartet_four_kernel(tc, query, keys_words, keys_scales, notes_wo
             nc.vector.tensor_tensor(cols(hi2, h), cols(picked["c"], h), cols(picked["d"], h), ALU.max)
         for h in range(2):
             nc.vector.tensor_tensor(cols(r, h), cols(hi1, h), cols(hi2, h), ALU.min)
+        lead = 128
+        nc.vector.tensor_copy(out=f2[:].indirect(lists["d"][:, :lead // 16]), in_=r[:, :lead])
         nc.vector.tensor_copy(out=f1[:].indirect(lists["a"][:]), in_=r[:])
-        nc.vector.tensor_copy(out=f2[:].indirect(lists["d"][:]), in_=r[:])
+        nc.vector.tensor_copy(out=f2[:].indirect(lists["d"][:, lead // 16:]), in_=r[:, lead:])
 
         aa = sb.tile([P, COLS], F32, name="aa")
         dd = sb.tile([P, COLS], F32, name="dd")
@@ -128,7 +130,8 @@ def tile_attend_quartet_four_kernel(tc, query, keys_words, keys_scales, notes_wo
         y0 = sb.tile([P, HALF], F32, name="y0")
         y1 = sb.tile([P, HALF], F32, name="y1")
         nc.gpsimd.tensor_tensor(aa[:], score["a"][:], f1[:], ALU.subtract)
-        nc.scalar.activation(out=left[:], in_=aa[:].indirect(lists["aa"][:]), func=COPY)
+        for h in range(2):
+            nc.scalar.activation(out=cols(left, h), in_=aa[:].indirect(half("aa", h)), func=COPY)
         cut = 768
         nc.gpsimd.tensor_tensor(dd[:, cut:], score["d"][:, cut:], f2[:, cut:], ALU.add)
         nc.vector.tensor_tensor(dd[:, :BANK], banks["d", 0][:], f2[:, :BANK], ALU.add)

@@ -90,7 +90,7 @@ def tile_attend_quartet_four_kernel(tc, query, keys_words, keys_scales, notes_wo
         hi2 = sb.tile([P, SLOTS], F32, name="hi2")
         r = sb.tile([P, SLOTS], F32, name="r")
         banks = {}
-        bank_tags = {"a": (0, 1), "b": (2, 3), "d": (4, 5), "c": (6, 7, 0, 1)}
+        bank_tags = {"a": (0, 1), "b": (2, 3, 4, 5), "d": (6, 7), "c": (0, 1, 2, 3)}
         for name in "abdc":
             w_in, s_in, fmt, width, row0 = pools[name]
             score[name] = sb.tile([P, COLS], F32, name="score_" + name)

from contextlib import ExitStack

import concourse.mybir as mybir

F32 = mybir.dt.float32
BF16 = mybir.dt.bfloat16
I32 = mybir.dt.int32
U32 = mybir.dt.uint32
U16 = mybir.dt.uint16
U8 = mybir.dt.uint8
FP8X4 = mybir.dt.float8_e4m3fn_x4
FP4X4 = mybir.dt.float4_e2m1fn_x4
ALU = mybir.AluOpType
COPY = mybir.ActivationFunctionType.Copy

P = 128
PACK = 4
D, COLS, SLOTS, Q = 512, 1024, 512, 128
BANK = 512
HALF = SLOTS // 2
FLOPS = 4 * 2 * D * Q * COLS


def tile_attend_quartet_four_kernel(tc, query, keys_words, keys_scales, notes_words, notes_scales,
                                     users_words, users_scales, shelves_words, shelves_scales,
                                     offs, offs2, offs3, offs4, offs5, offs6, out):
    nc = tc.nc
    with ExitStack() as ctx:
        sb = ctx.enter_context(tc.tile_pool(name="sb", bufs=1))
        ps = ctx.enter_context(tc.psum_pool(name="ps", bufs=1))

        pools = {
            "a": (keys_words[0], keys_scales[0], FP4X4, 2, 0),
            "b": (notes_words[0].rearrange("p n t -> p (n t)"), notes_scales[0], FP8X4, 4, 4),
            "c": (users_words[0], users_scales[0], FP4X4, 2, 0),
            "d": (shelves_words[0].rearrange("p n t -> p (n t)"), shelves_scales[0], FP8X4, 4, 8),
        }
        planes = {}
        words = {}
        for name in "abdc":
            planes[name] = sb.tile([P, COLS], U8, name="plane_" + name, align_bytes=64)
            words[name] = sb.tile([P, pools[name][3] * COLS], U8, name="words_" + name, align_bytes=64)
            nc.vector.memset(planes[name][:].bitcast(I32), 0)
        f1 = sb.tile([P, COLS], F32, name="f1")
        nc.vector.memset(f1[:], 0.0)

        lists = {}
        list_in = {"a": offs, "b": offs2, "c": offs3, "d": offs4, "aa": offs5, "dd": offs6}
        for name in list_in:
            lists[name] = sb.tile([P, SLOTS // 16], U16, name="list_" + name)

        def half(name, h):
            return lists[name][:, h * (HALF // 16):(h + 1) * (HALF // 16)]

        def load_words(name):
            nc.sync.dma_start(out=words[name][:].bitcast(I32), in_=pools[name][0].bitcast(I32))

        def load_scales(name, queue):
            rows = pools[name][1].rearrange("(g r) n -> r g n", r=4)
            row0 = pools[name][4]
            for r in range(4):
                queue.dma_start(out=planes[name][row0 + r:P:32, :].bitcast(I32), in_=rows[r].bitcast(I32))

        q_raw = sb.tile([P, PACK, Q], F32, name="q_raw")
        nc.sync.dma_start(out=q_raw[:], in_=query.rearrange("(p t) q -> p t q", t=PACK))
        load_scales("a", nc.sync)
        load_words("a")
        for before, name in zip("abd", "bdc"):
            load_words(name)
            load_scales(name, nc.sync)
            nc.sync.dma_start(lists[before][:], list_in[before])
        for name in ("c", "aa", "dd"):
            nc.sync.dma_start(lists[name][:], list_in[name])

        q_grp = sb.tile([P, Q, PACK], BF16, name="q_grp", tag="q_grp_f2", align_bytes=64)
        q_codes = sb.tile([P, Q], U32, name="q_codes", align_bytes=64)
        q_plane = sb.tile([P, Q], U8, name="q_plane", align_bytes=64)
        nc.vector.tensor_copy(out=q_grp[:], in_=q_raw[:].rearrange("p t q -> p q t"))
        nc.vector.quantize_mx(out=q_codes[:].bitcast(FP8X4), scales=q_plane[:],
                              in_=q_grp[:].rearrange("p q t -> p (q t)"))
        f2 = sb.tile([P, COLS], F32, name="f2", tag="q_grp_f2", align_bytes=64)
        nc.vector.memset(f2[:], 0.0)

        def cols(t, h):
            return t[:, HALF * h:HALF * (h + 1)]

        score = {}
        picked = {}
        hi1 = sb.tile([P, SLOTS], F32, name="hi1")
        hi2 = sb.tile([P, SLOTS], F32, name="hi2")
        r = sb.tile([P, SLOTS], F32, name="r")
        banks = {}
        bank_tags = {"a": (0, 1), "b": (2, 3, 4, 5), "d": (6, 7), "c": (0, 1, 2, 3)}
        for name in "abdc":
            w_in, s_in, fmt, width, row0 = pools[name]
            score[name] = sb.tile([P, COLS], F32, name="score_" + name)
            picked[name] = sb.tile([P, SLOTS], F32, name="picked_" + name)
            n = COLS // len(bank_tags[name])
            for j, tag in enumerate(bank_tags[name]):
                bank = ps.tile([P, n], F32, name="bank", tag="bank_%d" % tag)
                banks[name, j] = bank
                nc.tensor.matmul_mx(
                    out=bank[:],
                    lhsT=q_codes[:].bitcast(FP8X4), lhsT_scale=q_plane[:],
                    rhs=words[name][:, width * n * j:width * n * (j + 1)].bitcast(fmt),
                    rhs_scale=planes[name][row0:P, n * j:n * (j + 1)],
                    start=True, stop=True)
                dst = score[name][:, n * j:n * (j + 1)]
                if j % 2 == 0:
                    nc.vector.tensor_copy(out=dst, in_=bank[:])
                else:
                    nc.scalar.activation(out=dst, in_=bank[:], func=COPY)
            nc.vector.tensor_copy(out=cols(picked[name], 0), in_=score[name][:].indirect(half(name, 0)))
            nc.scalar.activation(out=cols(picked[name], 1), in_=score[name][:].indirect(half(name, 1)), func=COPY)
            if name == "b":
                nc.vector.tensor_tensor(hi1[:], picked["a"][:], picked["b"][:], ALU.max)
        for h in range(2):
            nc.vector.tensor_tensor(cols(hi2, h), cols(picked["c"], h), cols(picked["d"], h), ALU.max)
        for h in range(2):
            nc.vector.tensor_tensor(cols(r, h), cols(hi1, h), cols(hi2, h), ALU.min)
        lead = 128
        nc.vector.tensor_copy(out=f2[:].indirect(lists["d"][:, :lead // 16]), in_=r[:, :lead])
        nc.vector.tensor_copy(out=f1[:].indirect(lists["a"][:]), in_=r[:])
        nc.vector.tensor_copy(out=f2[:].indirect(lists["d"][:, lead // 16:]), in_=r[:, lead:])

        aa = sb.tile([P, COLS], F32, name="aa")
        dd = sb.tile([P, COLS], F32, name="dd")
        left = sb.tile([P, SLOTS], F32, name="left")
        stand = sb.tile([P, HALF], F32, name="stand")
        y0 = sb.tile([P, HALF], F32, name="y0")
        y1 = sb.tile([P, HALF], F32, name="y1")
        nc.gpsimd.tensor_tensor(aa[:], score["a"][:], f1[:], ALU.subtract)
        for h in range(2):
            nc.scalar.activation(out=cols(left, h), in_=aa[:].indirect(half("aa", h)), func=COPY)
        cut = 768
        nc.gpsimd.tensor_tensor(dd[:, cut:], score["d"][:, cut:], f2[:, cut:], ALU.add)
        nc.vector.tensor_tensor(dd[:, :BANK], banks["d", 0][:], f2[:, :BANK], ALU.add)
        nc.vector.tensor_tensor(dd[:, BANK:cut], banks["d", 1][:, :cut - BANK], f2[:, BANK:cut], ALU.add)
        nc.vector.tensor_tensor(y0[:], dd[:].indirect(half("dd", 0)), cols(left, 0), ALU.add)
        nc.scalar.activation(out=stand[:], in_=dd[:].indirect(half("dd", 1)), func=COPY)
        nc.vector.tensor_tensor(y1[:], stand[:], cols(left, 1), ALU.add)
        nc.sync.dma_start(out=out[:, 0:HALF], in_=y0[:])
        nc.scalar.dma_start(out=out[:, HALF:SLOTS], in_=y1[:])
